import numpy as np
import ml_dtypes


def mxq(x, axis, fmt="e4m3"):
    dtype, down = {"e4m3": (ml_dtypes.float8_e4m3fn, 7), "e5m2": (ml_dtypes.float8_e5m2, 14)}[fmt]
    v = np.moveaxis(np.asarray(x, np.float32).astype(ml_dtypes.bfloat16).astype(np.float64), axis, -1)
    blocks = v.reshape(v.shape[:-1] + (-1, 32))
    amax = np.abs(blocks).max(-1, keepdims=True)
    byte = np.maximum(np.where(amax > 0, np.frexp(amax)[1] - 1 + 127, 0) - down, 1)
    scale = np.exp2(byte - 127.0)
    codes = (blocks / scale).astype(np.float32).astype(dtype).astype(np.float64)
    return np.moveaxis((codes * scale).reshape(v.shape), -1, axis)


WIDE = False


def mx_kscale(k):
    if not WIDE:
        return np.ones(k)
    levels = np.array([10, -10, 5, -5, 0])
    if k % 512:
        return np.exp2(np.random.permutation(np.resize(levels, k // 32))).repeat(32)
    a = np.empty((k // 512, 16))
    for p in range(k // 512):
        a[p, :8] = np.random.permutation(np.resize(levels, 8))
        for g in range(8):
            far = levels[np.abs(levels - a[p, g]) >= 10]
            a[p, g + 8] = far[np.random.randint(len(far))]
    return np.exp2(a.ravel()).repeat(32)


BF16 = ml_dtypes.bfloat16


def bf(x):
    return np.asarray(x, np.float32).astype(BF16)


def f64(x):
    return np.asarray(x).astype(np.float64)


E2M1 = np.array([0.0, 0.5, 1.0, 1.5, 2.0, 3.0, 4.0, 6.0, -0.0, -0.5, -1.0, -1.5, -2.0, -3.0, -4.0, -6.0])


def pack_weight(w, fmt):
    k, n = w.shape
    w = f64(bf(w)).reshape(k // 32, 32, n)
    amax = np.abs(w).max(1)
    if fmt == "e4m3":
        byte = np.frexp(amax)[1] - 1 + 127 - 7
    else:
        mant, ex = np.frexp(amax / 6.0)
        byte = np.where(mant > 0.5, ex, ex - 1) + 127
    byte = np.clip(np.where(amax > 0, byte, 1), 1, 254)
    scaled = (w * np.exp2(127.0 - byte)[:, None, :]).reshape(k, n).astype(np.float32)
    by_word = np.ascontiguousarray(scaled.reshape(k // 512, 128, 4, n).transpose(0, 1, 3, 2))
    if fmt == "e4m3":
        words = by_word.astype(ml_dtypes.float8_e4m3fn).view(np.uint8)
    else:
        c = by_word.astype(ml_dtypes.float4_e2m1fn).view(np.uint8) & 0xF
        words = c[..., 0::2] | (c[..., 1::2] << 4)
    return np.ascontiguousarray(words), np.ascontiguousarray(byte.astype(np.uint8).reshape(k // 512, 16, n))


def unpack_weight(words, scales, fmt):
    g, p, n, _ = words.shape
    if fmt == "e4m3":
        vals = np.ascontiguousarray(words).view(ml_dtypes.float8_e4m3fn).astype(np.float64)
    else:
        nib = np.empty((g, p, n, 4), np.uint8)
        nib[..., 0::2] = words & 0xF
        nib[..., 1::2] = words >> 4
        vals = E2M1[nib]
    vals = vals * np.repeat(np.exp2(scales.astype(np.float64) - 127.0), 8, axis=1)[..., None]
    return vals.transpose(0, 1, 3, 2).reshape(g * 512, n)
def pack4(w):
    words, scales = pack_weight(w, "e2m1")
    return words.reshape(words.shape[0], 128, -1), scales


def unpack4(words, scales):
    return unpack_weight(words.reshape(words.shape[0], 128, -1, 2), scales, "e2m1")


def planes(Y):
    n, m = Y.shape
    b = f64(bf(Y)).reshape(n // 32, 32, m)
    amax = np.abs(b).max(1)
    byte = np.clip(np.where(amax > 0, np.frexp(amax)[1] - 1 + 127 - 7, 1), 1, 254)
    codes = (b * np.exp2(127.0 - byte)[:, None, :]).reshape(n, m).astype(np.float32).astype(ml_dtypes.float8_e4m3fn).view(np.uint8)
    words = codes.reshape(n // 512, 128, 4, m).transpose(0, 1, 3, 2)
    return np.ascontiguousarray(words), np.ascontiguousarray(byte.astype(np.uint8).reshape(n // 512, 16, m))


S, T, V, D, F = 768, 512, 2048, 1024, 1536


def setup_inputs():
    a = mx_kscale(T)
    u = mx_kscale(V)
    t = mx_kscale(D)
    P = np.random.exponential(size=(S, T)) / np.sqrt(2 * T)
    H = np.random.randn(T, D)
    C = np.random.exponential(size=(S, V)) / np.sqrt(2 * V)
    E = np.random.randn(V, D)
    W = np.random.randn(D, F) / np.sqrt(2 * D)
    e_words, e_scales = pack4(E * u[:, None] * t[None, :])
    return {
        "pool": bf(P / a[None, :]),
        "states": bf(H * a[:, None] * t[None, :]),
        "word_pool": bf(C / u[None, :]),
        "e_words": e_words,
        "e_scales": e_scales,
        "dense": bf(W / t[:, None]),
        "bias": bf(0.3 * np.random.randn(F)),
        "feat_scale": bf(np.exp(0.8 * np.random.randn(F))),
        "sent_scale": bf(np.exp(0.3 * np.random.randn(S))),
    }

def reference(pool, states, word_pool, e_words, e_scales, dense, bias, feat_scale, sent_scale):
    ctx = mxq(f64(pool), 1, "e4m3") @ mxq(f64(states), 0, "e4m3")
    words_part = mxq(f64(word_pool), 1, "e4m3") @ unpack4(e_words, e_scales)
    pooled = ctx + words_part
    z = mxq(pooled, 1, "e4m3") @ mxq(f64(dense), 0, "e4m3")
    h = np.tanh(z + f64(bias)[None, :])
    y = h * f64(feat_scale)[None, :] * f64(sent_scale)[:, None]
    Y = y.T
    words, scales = planes(Y)
    return y, words, scales

from contextlib import ExitStack

import concourse.mybir as mybir
from concourse.masks import make_identity

S, T, V, D, F = 768, 512, 2048, 1024, 1536
FLOPS = 2 * S * (T + V) * D + 2 * S * D * F

F32 = mybir.dt.float32
BF16 = mybir.dt.bfloat16
I32 = mybir.dt.int32
U32 = mybir.dt.uint32
U8 = mybir.dt.uint8
FP8X4 = mybir.dt.float8_e4m3fn_x4
FP4X4 = mybir.dt.float4_e2m1fn_x4
ADD = mybir.AluOpType.add
MULT = mybir.AluOpType.mult
TANH = mybir.ActivationFunctionType.Tanh

P = 128
PACK = 4
KP = P * PACK
NT = S // P
GV = V // KP
GD = D // KP
GF = F // KP
X_BUFS = 3
Y_BUFS = 6
E_BUFS = 3
R_BUFS = 6
DENSE_ON_SCALAR = [(2, 0)]
CAST_ON_SCALAR = [0, 1, 3, 4, 7, 9, 10, 12, 14, 15, 17]
TURN_BANKS = 3
Z_BANKS = 3
LOADS = "p0 w0 sc s1 e0 e1 s0 w1 p1 w2 d11 d01 p3 p2 w3 d00 d20 d10 w4 w5 p5 d21 p4"
ORDER = "w0 G1 G0 p0 v E01 D01 E00 w1 D11 D00 p1 S01 S00 w2 A11 p2 P0 p3 A10 w3 P1 A20 D10 Z00 A21 Z10 D20 A30 P2 w4 Z01 A31 Y00 p4 Y10 Z11 D21 Z02 Z12 P3 Y01 Z21 A40 w5 Y11 Z20 A41 p5 Y12 Z31 Y02 Z30 P4 Z32 Y20 Z22 A50 Y21 Z40 A51 Z41 P5 Y31 Z42 Y22 Y32 Y30 Y40 Z52 Y41 Z50 Y42 Z51 Y52 Y50 Y51"


def tile_pooled_sentence_tanh_dense_k6_kernel(
    tc, pool, states, word_pool, e_words, e_scales, dense, bias, feat_scale, sent_scale, out_0, out_1, out_2
):
    nc = tc.nc
    with ExitStack() as ctx:
        sb = ctx.enter_context(tc.tile_pool(name="sb", bufs=1))
        ps = ctx.enter_context(tc.psum_pool(name="ps", bufs=1))
        ctx.enter_context(tc.manual_schedule(engines={mybir.EngineType.PE}))

        def tiles(name, count, shape, dtype):
            return [sb.tile(shape, dtype, name="%s%d" % (name, n), align_bytes=64) for n in range(count)]

        def one(name, shape, dtype):
            return sb.tile(shape, dtype, name=name, align_bytes=64)

        turn_banks = [ps.tile([P, 4, P], F32, name="turn%d" % n) for n in range(TURN_BANKS)]
        pooled_banks = [ps.tile([P, KP], F32, name="acc_pooled%d" % n) for n in range(GD)]
        z_banks = [ps.tile([P, KP], F32, name="acc_z%d" % n) for n in range(Z_BANKS)]

        ident = one("ident", [P, P], F32)
        wp_raw = tiles("wp_raw", NT, [P, V], BF16)
        pool_raw = tiles("pool_raw", NT, [P, T], BF16)
        wp_turned = tiles("wp_turned", 2, [P, GV, P, PACK], BF16)
        pool_turned = tiles("pool_turned", 2, [P, 1, P, PACK], BF16)
        x_codes = tiles("x_codes", X_BUFS, [P, GV + 1, P], U32)
        x_scales = tiles("x_scales", X_BUFS, [P, GV + 1, P], U8)
        states_raw = tiles("states_raw", GD, [P, PACK, KP], BF16)
        states_codes = one("states_codes", [P, D], U32)
        states_scales = one("states_scales", [P, D], U8)
        table_words = one("table_words", [P, GV, 2 * D], U8)
        table_scales = one("table_scales", [P, GV, D], U8)
        dense_raw = tiles("dense_raw", GF * GD, [P, PACK, KP], BF16)
        grouped = tiles("grouped", 8, [P, KP, PACK], BF16)
        dense_codes = one("dense_codes", [P, GF, GD, KP], U32)
        dense_scales = one("dense_scales", [P, GF, GD, KP], U8)
        vec_head = tiles("vec_head", 2, [P, 8], BF16)
        vec_tail = tiles("vec_tail", 2, [P, 4], BF16)
        spread = one("spread", [P, 2, F], BF16)
        sent_rows = one("sent_rows", [NT, P], BF16)
        sent_wide = one("sent_wide", [P, P], F32)
        sent_cols = one("sent_cols", [P, NT], F32)
        pooled = tiles("pooled", 2, [P, GD, 2, P, 2], BF16)
        pooled_turned = tiles("pooled_turned", 2, [P, GD, P, PACK], BF16)
        pooled_codes = tiles("pooled_codes", NT, [P, GD, P], U32)
        pooled_scales = tiles("pooled_scales", NT, [P, GD, P], U8)
        biased = tiles("biased", E_BUFS, [P, KP], F32)
        squashed = tiles("squashed", E_BUFS, [P, KP], F32)
        y = tiles("y", Y_BUFS, [P, KP], F32)
        y_rounded = tiles("y_rounded", R_BUFS, [P, 2, P, 2], BF16)
        y_turned = tiles("y_turned", R_BUFS, [P, 1, P, PACK], BF16)
        y_codes = one("y_codes", [P, GF, S], U32)
        y_scales = one("y_scales", [P, GF, S], U8)
        out_words = out_1.rearrange("g p m t -> p g (m t)").bitcast(I32)

        turn_count = []

        def next_turn_bank():
            turn_count.append(1)
            return turn_banks[len(turn_count) % len(turn_banks)]

        def rows(i):
            return slice(i * P, (i + 1) * P)

        def chunk(c):
            return slice(c * KP, (c + 1) * KP)

        def load(name):
            kind = name[0]
            if name == "sc":
                for q in range(4):
                    nc.sync.dma_start(
                        out=table_scales[32 * q : 32 * q + 4].bitcast(I32),
                        in_=e_scales[:, 4 * q : 4 * q + 4, :].rearrange("g r n -> r g n").bitcast(I32),
                    )
            elif kind == "w":
                nc.sync.dma_start(out=wp_raw[int(name[1])][:], in_=word_pool[rows(int(name[1])), :])
            elif kind == "p":
                nc.sync.dma_start(out=pool_raw[int(name[1])][:], in_=pool[rows(int(name[1])), :])
            elif kind == "s":
                h = int(name[1])
                nc.sync.dma_start(out=states_raw[h][:], in_=states[:, chunk(h)].rearrange("(p j) n -> p j n", j=PACK))
            elif kind == "e":
                half = slice(2 * int(name[1]), 2 * int(name[1]) + 2)
                nc.sync.dma_start(out=table_words[:, half].bitcast(I32), in_=e_words[half].rearrange("g p n -> p g n").bitcast(I32))
            else:
                c, g = int(name[1]), int(name[2])
                nc.sync.dma_start(
                    out=dense_raw[c * GD + g][:], in_=dense[chunk(g), chunk(c)].rearrange("(p j) n -> p j n", j=PACK)
                )

        def interleave(on_scalar, dst, raw):
            out = dst[:].rearrange("p (c i) t -> p c t i", i=4)
            src = raw[:].rearrange("p t (c i) -> p c t i", i=4)
            if on_scalar:
                nc.scalar.copy(out=out, in_=src)
            else:
                nc.vector.tensor_copy(out=out, in_=src)

        def quantise(codes, scales, src):
            nc.vector.quantize_mx(out=codes.bitcast(FP8X4), scales=scales, in_=src)

        def group_states(h):
            interleave(False, grouped[h], states_raw[h])

        def quantise_states(h):
            quantise(states_codes[:, chunk(h)], states_scales[:, chunk(h)], grouped[h][:].rearrange("p n t -> p (n t)"))

        def group_dense(c, g):
            interleave((c, g) in DENSE_ON_SCALAR, grouped[c * GD + g + 2], dense_raw[c * GD + g])

        def quantise_dense(c, g):
            quantise(dense_codes[:, c, g, :], dense_scales[:, c, g, :], grouped[c * GD + g + 2][:].rearrange("p n t -> p (n t)"))

        def turn(jobs):
            for first in range(0, len(jobs), 2):
                bank = next_turn_bank()
                pair = jobs[first : first + 2]
                for slot, job in enumerate(pair):
                    for u in range(2):
                        nc.tensor.transpose(bank[:, 2 * slot + u, :], job[0][u], ident[:])
                if len(pair) == 2 and pair[0][1] is pair[1][1]:
                    spans = [(0, 2)]
                else:
                    spans = [(slot, 1) for slot in range(len(pair))]
                for slot, count in spans:
                    dst, g = pair[slot][1], pair[slot][2]
                    nc.scalar.copy(
                        out=dst[:, g : g + count].bitcast(F32),
                        in_=bank[:, 2 * slot : 2 * (slot + count), :].rearrange("p (g u) s -> p g s u", u=2),
                    )
                for job in pair:
                    if job[3] is not None:
                        job[3]()

        def flat(ap):
            return ap.rearrange("p g s -> p (g s)")

        def wp_jobs(i):
            words = wp_raw[i][:].bitcast(F32)
            dst = wp_turned[i % 2]

            def after():
                quantise(flat(x_codes[i % X_BUFS][:, 0:GV, :]), flat(x_scales[i % X_BUFS][:, 0:GV, :]), dst[:].rearrange("p g s t -> p (g s t)"))

            return [
                ([words[:, 256 * g + u : 256 * (g + 1) : 2] for u in range(2)], dst, g, after if g == GV - 1 else None)
                for g in range(GV)
            ]

        def pool_jobs(i):
            words = pool_raw[i][:].bitcast(F32)
            dst = pool_turned[i % 2]

            def after():
                quantise(x_codes[i % X_BUFS][:, GV, :], x_scales[i % X_BUFS][:, GV, :], dst[:].rearrange("p g s t -> p (g s t)"))

            return [([words[:, u:256:2] for u in range(2)], dst, 0, after)]

        def pooled_jobs(i):
            words = pooled[i % 2][:].bitcast(F32)
            dst = pooled_turned[i % 2]

            def after():
                quantise(flat(pooled_codes[i][:]), flat(pooled_scales[i][:]), dst[:].rearrange("p g s t -> p (g s t)"))

            return [([words[:, g, u, :, 0] for u in range(2)], dst, g, after if g == GD - 1 else None) for g in range(GD)]

        def y_jobs(i, c):
            n = item_number[(i, c)]
            words = y_rounded[n % R_BUFS][:].bitcast(F32)
            dst = y_turned[n % R_BUFS]

            def after():
                quantise(y_codes[:, c, rows(i)], y_scales[:, c, rows(i)], dst[:].rearrange("p g s t -> p (g s t)"))
                done.add((i, c))
                if i == NT - 1:
                    if len(done) == NT * GF:
                        store_scales(NT - 1, NT)
                    nc.sync.dma_start(out=out_words[:, c, rows(i)], in_=y_codes[:, c, rows(i)].bitcast(I32))
                elif all((i, cc) in done for cc in range(GF)):
                    nc.sync.dma_start(out=out_words[:, :, rows(i)], in_=y_codes[:, :, rows(i)].bitcast(I32))
                    if all((ii, cc) in done for ii in range(NT - 1) for cc in range(GF)):
                        store_scales(0, NT - 1)

            return [([words[:, u, :, 0] for u in range(2)], dst, 0, after)]

        def stage_one(i, h, passes):
            codes, scales = x_codes[i % X_BUFS], x_scales[i % X_BUFS]
            for g in passes:
                if g < GV:
                    rhs = table_words[:, g, 2 * KP * h : 2 * KP * (h + 1)].bitcast(FP4X4)
                    rhs_scale = table_scales[:, g, chunk(h)]
                else:
                    rhs = states_codes[:, chunk(h)].bitcast(FP8X4)
                    rhs_scale = states_scales[:, chunk(h)]
                nc.tensor.matmul_mx(
                    out=pooled_banks[h][:], lhsT=codes[:, g, :].bitcast(FP8X4), lhsT_scale=scales[:, g, :],
                    rhs=rhs, rhs_scale=rhs_scale, start=(g == 0), stop=(g == GV),
                )
            if GV in passes:
                nc.scalar.copy(out=pooled[i % 2][:, h], in_=pooled_banks[h][:].rearrange("s (p u e) -> s u p e", u=2, e=2))

        item_number = {}
        done = set()

        def stage_two(i, c):
            n = len(item_number)
            item_number[(i, c)] = n
            bank = z_banks[n % Z_BANKS]
            for g in range(GD):
                nc.tensor.matmul_mx(
                    out=bank[:], lhsT=pooled_codes[i][:, g, :].bitcast(FP8X4), lhsT_scale=pooled_scales[i][:, g, :],
                    rhs=dense_codes[:, c, g, :].bitcast(FP8X4), rhs_scale=dense_scales[:, c, g, :],
                    start=(g == 0), stop=(g == GD - 1),
                )
            nc.vector.tensor_tensor(out=biased[n % E_BUFS][:], in0=bank[:], in1=spread[:, 0, chunk(c)], op=ADD)
            nc.scalar.activation(out=squashed[n % E_BUFS][:], in_=biased[n % E_BUFS][:], func=TANH)
            nc.vector.scalar_tensor_tensor(
                out=y[n % Y_BUFS][:], in0=squashed[n % E_BUFS][:], scalar=sent_cols[:, i : i + 1],
                in1=spread[:, 1, chunk(c)], op0=MULT, op1=MULT,
            )
            nc.sync.dma_start(out=out_0[rows(i), chunk(c)], in_=y[n % Y_BUFS][:])
            src = y[n % Y_BUFS][:].rearrange("s (p u e) -> s u p e", u=2, e=2)
            if i * GF + c in CAST_ON_SCALAR:
                nc.scalar.copy(out=y_rounded[n % R_BUFS][:], in_=src)
            else:
                nc.vector.tensor_copy(out=y_rounded[n % R_BUFS][:], in_=src)

        def store_scales(first, last):
            cols = slice(first * P, last * P)
            for q in range(4):
                nc.sync.dma_start(
                    out=out_2[:, 4 * q : 4 * q + 4, cols].rearrange("g r m -> r g m").bitcast(I32),
                    in_=y_scales[32 * q : 32 * q + 4, :, cols].bitcast(I32),
                )

        vec_banks = z_banks

        def spread_vectors():
            for v in range(2):
                words = vec_head[v][:].bitcast(F32)
                bank = vec_banks[v][:].rearrange("p (c n) -> p c n", c=4)
                for c in range(4):
                    nc.tensor.transpose(bank[:, c, :], words[:, c : c + 1].to_broadcast([P, P]), ident[:])
            bank = vec_banks[2][:].rearrange("p (v c n) -> p v c n", v=2, c=2)
            for v in range(2):
                words = vec_tail[v][:].bitcast(F32)
                for c in range(2):
                    nc.tensor.transpose(bank[:, v, c, :], words[:, c : c + 1].to_broadcast([P, P]), ident[:])
            bank = next_turn_bank()
            nc.tensor.transpose(bank[:, 0, :], sent_wide[:], ident[:])
            return bank

        def leave_vectors(bank):
            nc.scalar.copy(out=sent_cols[:], in_=bank[:, 0, 0:NT])
            words = spread[:].bitcast(F32)
            for v in range(2):
                nc.scalar.copy(
                    out=words[:, v, 0:KP].rearrange("p (n c) -> p n c", c=4),
                    in_=vec_banks[v][:].rearrange("p (c n) -> p n c", c=4),
                )
            nc.scalar.copy(
                out=words[:, :, KP : F // 2].rearrange("p v (n c) -> p v n c", c=2),
                in_=vec_banks[2][:].rearrange("p (v c n) -> p v n c", v=2, c=2),
            )

        nc.vector.memset(table_scales[:].bitcast(I32), 0)
        make_identity(nc, ident[:])
        nc.gpsimd.memset(sent_wide[:], 0.0)
        nc.scalar.dma_start(out=sent_rows[:], in_=sent_scale.rearrange("(i p) -> i p", p=P))
        for v, vec in enumerate((bias, feat_scale)):
            nc.scalar.dma_start(out=vec_head[v][:], in_=vec[0 : 8 * P].rearrange("(p c) -> p c", c=8))
            nc.scalar.dma_start(out=vec_tail[v][:], in_=vec[8 * P : F].rearrange("(p c) -> p c", c=4))
        for name in LOADS.split():
            load(name)
        nc.scalar.activation(out=squashed[0][:, 0:1], in_=ident[:, 0:1], func=TANH)

        nc.vector.tensor_copy(out=sent_wide[0:NT, :], in_=sent_rows[:])
        jobs = []
        for token in ORDER.split():
            kind, i, c = token[0], int((token + "00")[1]), int((token + "00")[2])
            if kind in "wpPY":
                jobs.extend({"w": wp_jobs, "p": pool_jobs, "P": pooled_jobs}[kind](i) if kind != "Y" else y_jobs(i, c))
                continue
            if kind == "D":
                group_dense(i, c)
                quantise_dense(i, c)
                continue
            if kind == "G":
                group_states(i)
                quantise_states(i)
                continue
            turn(jobs)
            jobs = []
            if kind == "v":
                leave_vectors(spread_vectors())
            elif kind == "E":
                stage_one(i, c, range(GV))
            elif kind == "S":
                stage_one(i, c, [GV])
            elif kind == "A":
                stage_one(i, c, range(GV + 1))
            elif kind == "Z":
                stage_two(i, c)
        turn(jobs)
